import numpy as np
import ml_dtypes

BF16 = ml_dtypes.bfloat16


def bf(x):
    return np.asarray(x, np.float32).astype(BF16)


def f32(x):
    return np.asarray(x, np.float32)


def f64(x):
    return np.asarray(x).astype(np.float64)


def striped(idx):
    return np.tile(idx.reshape(-1, 16).T, (8, 1))


def rows(idx, k):
    return np.tile(idx, (k, 1))


def look(tab, idx):
    return np.take_along_axis(f64(tab), rows(idx, len(tab)), axis=1)


K, S, V, N, M = 512, 2048, 2048, 2048, 512


def setup_inputs():
    return {"tab": f32(np.random.standard_normal((K, S))), "pos": f32(np.random.standard_normal((K, V))), "w": bf(np.random.standard_normal((K, M)) / np.sqrt(K)), "b": f32(0.5 * np.random.standard_normal((M, 1))), "offs": striped(np.random.permutation(S)[:N])}


def reference(tab, pos, w, b, offs):
    idx = offs[:16].T.reshape(-1)
    x = np.maximum(look(tab, idx) - f64(pos) + 0.5, 0.0)
    y = f64(w).T @ x
    return np.maximum(y + f64(b), 0.0)

@@ -1,0 +1,80 @@
+import concourse.mybir as mybir
+
+F32, BF16, U16 = mybir.dt.float32, mybir.dt.bfloat16, mybir.dt.uint16
+subtract = mybir.AluOpType.subtract
+Relu = mybir.ActivationFunctionType.Relu
+
+P = 128
+BANK = 512
+GROUP = 1024
+MARGIN = 0.5
+FLOPS = 2 * 512 * 512 * 2048
+
+
+def tile_lookup_hinge_sub_relu_kernel(tc, tab, pos, w, b, offs, out):
+    nc = tc.nc
+    K, S = tab.shape
+    M, N = out.shape
+    R, MB, G = K // P, M // P, N // GROUP
+    with (
+        tc.tile_pool(name="held", bufs=1) as held,
+        tc.tile_pool(name="diffs", bufs=3) as diffs,
+        tc.tile_pool(name="results", bufs=4) as results,
+        tc.psum_pool(name="psum", bufs=8) as psum,
+        nc.allow_non_contiguous_dma(reason="the bias is loaded one value to a partition"),
+    ):
+        offsets = held.tile([P, N // 16], U16, name="offsets")
+        tables = [held.tile([P, S], F32, name=f"table{r}") for r in range(R)]
+        positives = [held.tile([P, N], F32, name=f"positives{r}") for r in range(R)]
+        weights = held.tile([P, R, M], BF16, name="weights")
+        bias = held.tile([P, MB], F32, name="bias")
+        margin = held.tile([P, 1], F32, name="margin")
+
+        def load_positives(r, g):
+            cols = slice(g * GROUP, (g + 1) * GROUP)
+            nc.sync.dma_start(positives[r][:, cols], pos[r * P : (r + 1) * P, cols])
+
+        nc.sync.dma_start(offsets[:], offs)
+        for r in range(R):
+            nc.sync.dma_start(tables[r][:], tab[r * P : (r + 1) * P, :])
+            load_positives(r, 0)
+            if r == 0:
+                nc.sync.dma_start(weights[:], w.rearrange("(r p) m -> p r m", p=P))
+                nc.sync.dma_start(bias[:], b.rearrange("(m p) one -> p (m one)", p=P))
+        for g in range(1, G):
+            for r in range(R):
+                load_positives(r, g)
+        nc.gpsimd.memset(margin[:], MARGIN)
+
+        for g in range(G):
+            banks = [
+                [psum.tile([P, BANK], F32, name=f"bank_g{g}m{m}h{h}", tag="bank") for h in range(GROUP // BANK)]
+                for m in range(MB)
+            ]
+            for r in range(R):
+                cols = slice(g * GROUP, (g + 1) * GROUP)
+                diff = diffs.tile([P, GROUP], F32)
+                nc.vector.tensor_tensor(
+                    diff[:],
+                    tables[r][:].indirect(offsets[:, g * GROUP // 16 : (g + 1) * GROUP // 16]),
+                    positives[r][:, cols],
+                    subtract,
+                )
+                x = diffs.tile([P, GROUP], BF16)
+                nc.scalar.activation(x[:], diff[:], Relu, bias=margin[:])
+                for m in range(MB):
+                    for h in range(GROUP // BANK):
+                        nc.tensor.matmul(
+                            banks[m][h][:],
+                            weights[:, r, m * P : (m + 1) * P],
+                            x[:, h * BANK : (h + 1) * BANK],
+                            start=r == 0,
+                            stop=r == R - 1,
+                        )
+            for m in range(MB):
+                result = results.tile([P, GROUP], F32)
+                for h in range(GROUP // BANK):
+                    nc.scalar.activation(
+                        result[:, h * BANK : (h + 1) * BANK], banks[m][h][:], Relu, bias=bias[:, m : m + 1]
+                    )
+                nc.sync.dma_start(out[m * P : (m + 1) * P, g * GROUP : (g + 1) * GROUP], result[:])

@@ -1,12 +1,12 @@
 import concourse.mybir as mybir
 
 F32, BF16, U16 = mybir.dt.float32, mybir.dt.bfloat16, mybir.dt.uint16
-subtract = mybir.AluOpType.subtract
+subtract, add, maximum = mybir.AluOpType.subtract, mybir.AluOpType.add, mybir.AluOpType.max
 Relu = mybir.ActivationFunctionType.Relu
 
 P = 128
-BANK = 512
-GROUP = 1024
+GROUP = 512
+LOAD = 2 * GROUP
 MARGIN = 0.5
 FLOPS = 2 * 512 * 512 * 2048
 
@@ -18,8 +18,8 @@ def tile_lookup_hinge_sub_relu_kernel(tc, tab, pos, w, b, offs, out):
     R, MB, G = K // P, M // P, N // GROUP
     with (
         tc.tile_pool(name="held", bufs=1) as held,
-        tc.tile_pool(name="diffs", bufs=3) as diffs,
-        tc.tile_pool(name="results", bufs=4) as results,
+        tc.tile_pool(name="terms", bufs=4) as terms,
+        tc.tile_pool(name="results", bufs=8) as results,
         tc.psum_pool(name="psum", bufs=8) as psum,
         nc.allow_non_contiguous_dma(reason="the bias is loaded one value to a partition"),
     ):
@@ -29,52 +29,60 @@ def tile_lookup_hinge_sub_relu_kernel(tc, tab, pos, w, b, offs, out):
         weights = held.tile([P, R, M], BF16, name="weights")
         bias = held.tile([P, MB], F32, name="bias")
         margin = held.tile([P, 1], F32, name="margin")
+        nc.gpsimd.memset(margin[:], MARGIN)
 
-        def load_positives(r, g):
-            cols = slice(g * GROUP, (g + 1) * GROUP)
+        def load_positives(r, start):
+            cols = slice(start, start + LOAD)
             nc.sync.dma_start(positives[r][:, cols], pos[r * P : (r + 1) * P, cols])
 
         nc.sync.dma_start(offsets[:], offs)
         for r in range(R):
             nc.sync.dma_start(tables[r][:], tab[r * P : (r + 1) * P, :])
             load_positives(r, 0)
-            if r == 0:
+            if r == 1:
                 nc.sync.dma_start(weights[:], w.rearrange("(r p) m -> p r m", p=P))
-                nc.sync.dma_start(bias[:], b.rearrange("(m p) one -> p (m one)", p=P))
-        for g in range(1, G):
+        nc.sync.dma_start(bias[:], b.rearrange("(m p) one -> p (m one)", p=P))
+        for start in range(LOAD, N, LOAD):
             for r in range(R):
-                load_positives(r, g)
-        nc.gpsimd.memset(margin[:], MARGIN)
+                load_positives(r, start)
 
-        for g in range(G):
-            banks = [
-                [psum.tile([P, BANK], F32, name=f"bank_g{g}m{m}h{h}", tag="bank") for h in range(GROUP // BANK)]
-                for m in range(MB)
-            ]
-            for r in range(R):
-                cols = slice(g * GROUP, (g + 1) * GROUP)
-                diff = diffs.tile([P, GROUP], F32)
-                nc.vector.tensor_tensor(
-                    diff[:],
-                    tables[r][:].indirect(offsets[:, g * GROUP // 16 : (g + 1) * GROUP // 16]),
-                    positives[r][:, cols],
-                    subtract,
-                )
-                x = diffs.tile([P, GROUP], BF16)
-                nc.scalar.activation(x[:], diff[:], Relu, bias=margin[:])
-                for m in range(MB):
-                    for h in range(GROUP // BANK):
-                        nc.tensor.matmul(
-                            banks[m][h][:],
-                            weights[:, r, m * P : (m + 1) * P],
-                            x[:, h * BANK : (h + 1) * BANK],
-                            start=r == 0,
-                            stop=r == R - 1,
-                        )
+        banks = {}
+
+        def look_up(g, r):
+            cols = slice(g * GROUP, (g + 1) * GROUP)
+            diff = terms.tile([P, GROUP], F32)
+            nc.vector.tensor_tensor(
+                diff[:],
+                tables[r][:].indirect(offsets[:, g * GROUP // 16 : (g + 1) * GROUP // 16]),
+                positives[r][:, cols],
+                subtract,
+            )
+            x = terms.tile([P, GROUP], BF16, bufs=16)
+            nc.scalar.activation(x[:], diff[:], Relu, bias=margin[:])
             for m in range(MB):
-                result = results.tile([P, GROUP], F32)
-                for h in range(GROUP // BANK):
-                    nc.scalar.activation(
-                        result[:, h * BANK : (h + 1) * BANK], banks[m][h][:], Relu, bias=bias[:, m : m + 1]
-                    )
-                nc.sync.dma_start(out[m * P : (m + 1) * P, g * GROUP : (g + 1) * GROUP], result[:])
+                if r == 0:
+                    banks[g, m] = psum.tile([P, GROUP], F32, name=f"bank{g}_{m}", tag="bank")
+                nc.tensor.matmul(
+                    banks[g, m][:], weights[:, r, m * P : (m + 1) * P], x[:], start=r == 0, stop=r == R - 1
+                )
+
+        def finish(g, m):
+            result = results.tile([P, GROUP], F32)
+            if m == MB - 1 or (g == G - 1 and m == 1):
+                nc.vector.tensor_scalar(result[:], banks[g, m][:], bias[:, m : m + 1], 0.0, add, maximum)
+            else:
+                nc.scalar.activation(result[:], banks[g, m][:], Relu, bias=bias[:, m : m + 1])
+            nc.sync.dma_start(out[m * P : (m + 1) * P, g * GROUP : (g + 1) * GROUP], result[:])
+
+        order = [(g, r) for r in range(R) for g in (0, 1)] + [(g, r) for g in range(2, G) for r in range(R)]
+        waiting = []
+        for i, (g, r) in enumerate(order):
+            for tile in waiting[:2]:
+                finish(*tile)
+            waiting = waiting[2:]
+            look_up(g, r)
+            if i > 0 and order[i - 1][1] == R - 1:
+                waiting += [(order[i - 1][0], m) for m in range(MB)]
+        waiting += [(G - 1, m) for m in range(MB)]
+        for tile in waiting:
+            finish(*tile)

@@ -6,7 +6,7 @@ Relu = mybir.ActivationFunctionType.Relu
 
 P = 128
 GROUP = 512
-LOAD = 2 * GROUP
+BLOCK = 32
 MARGIN = 0.5
 FLOPS = 2 * 512 * 512 * 2048
 
@@ -21,30 +21,38 @@ def tile_lookup_hinge_sub_relu_kernel(tc, tab, pos, w, b, offs, out):
         tc.tile_pool(name="terms", bufs=4) as terms,
         tc.tile_pool(name="results", bufs=8) as results,
         tc.psum_pool(name="psum", bufs=8) as psum,
-        nc.allow_non_contiguous_dma(reason="the bias is loaded one value to a partition"),
     ):
         offsets = held.tile([P, N // 16], U16, name="offsets")
         tables = [held.tile([P, S], F32, name=f"table{r}") for r in range(R)]
         positives = [held.tile([P, N], F32, name=f"positives{r}") for r in range(R)]
         weights = held.tile([P, R, M], BF16, name="weights")
-        bias = held.tile([P, MB], F32, name="bias")
+        bias_rows = held.tile([P, BLOCK], F32, name="bias_rows", align_bytes=64)
+        bias = held.tile([P, BLOCK], F32, name="bias", align_bytes=64)
         margin = held.tile([P, 1], F32, name="margin")
         nc.gpsimd.memset(margin[:], MARGIN)
 
-        def load_positives(r, start):
-            cols = slice(start, start + LOAD)
+        def load_positives(r, start, width):
+            cols = slice(start, start + width)
             nc.sync.dma_start(positives[r][:, cols], pos[r * P : (r + 1) * P, cols])
+
+        nc.gpsimd.memset(bias_rows[:], 0.0)
+        b_rows = b.rearrange("(m q i) one -> q m (i one)", q=P // BLOCK, i=BLOCK)
+        for q in range(P // BLOCK):
+            nc.scalar.dma_start(bias_rows[q * BLOCK : q * BLOCK + MB, :], b_rows[q])
+        nc.vector.transpose(bias[:], bias_rows[:])
 
         nc.sync.dma_start(offsets[:], offs)
         for r in range(R):
             nc.sync.dma_start(tables[r][:], tab[r * P : (r + 1) * P, :])
-            load_positives(r, 0)
+            if r < R - 1:
+                load_positives(r, 0, 2 * GROUP)
+            else:
+                load_positives(r, 0, GROUP)
+                load_positives(r, GROUP, GROUP)
             if r == 1:
                 nc.sync.dma_start(weights[:], w.rearrange("(r p) m -> p r m", p=P))
-        nc.sync.dma_start(bias[:], b.rearrange("(m p) one -> p (m one)", p=P))
-        for start in range(LOAD, N, LOAD):
-            for r in range(R):
-                load_positives(r, start)
+        for r in range(R):
+            load_positives(r, 2 * GROUP, N - 2 * GROUP)
 
         banks = {}
 

@@ -5,8 +5,11 @@ subtract, add, maximum = mybir.AluOpType.subtract, mybir.AluOpType.add, mybir.Al
 Relu = mybir.ActivationFunctionType.Relu
 
 P = 128
-GROUP = 512
+BANK = 512
+WIDTHS = (BANK, BANK, BANK, BANK // 2, BANK // 2)
+EARLY = 2
 BLOCK = 32
+LAG = 2
 MARGIN = 0.5
 FLOPS = 2 * 512 * 512 * 2048
 
@@ -15,7 +18,9 @@ def tile_lookup_hinge_sub_relu_kernel(tc, tab, pos, w, b, offs, out):
     nc = tc.nc
     K, S = tab.shape
     M, N = out.shape
-    R, MB, G = K // P, M // P, N // GROUP
+    R, MB, G = K // P, M // P, len(WIDTHS)
+    starts = [sum(WIDTHS[:g]) for g in range(G)]
+    early_columns = starts[EARLY]
     with (
         tc.tile_pool(name="held", bufs=1) as held,
         tc.tile_pool(name="terms", bufs=4) as terms,
@@ -35,62 +40,66 @@ def tile_lookup_hinge_sub_relu_kernel(tc, tab, pos, w, b, offs, out):
             cols = slice(start, start + width)
             nc.sync.dma_start(positives[r][:, cols], pos[r * P : (r + 1) * P, cols])
 
-        nc.gpsimd.memset(bias_rows[:], 0.0)
-        b_rows = b.rearrange("(m q i) one -> q m (i one)", q=P // BLOCK, i=BLOCK)
-        for q in range(P // BLOCK):
-            nc.scalar.dma_start(bias_rows[q * BLOCK : q * BLOCK + MB, :], b_rows[q])
-        nc.vector.transpose(bias[:], bias_rows[:])
-
         nc.sync.dma_start(offsets[:], offs)
         for r in range(R):
             nc.sync.dma_start(tables[r][:], tab[r * P : (r + 1) * P, :])
             if r < R - 1:
-                load_positives(r, 0, 2 * GROUP)
+                load_positives(r, 0, early_columns)
             else:
-                load_positives(r, 0, GROUP)
-                load_positives(r, GROUP, GROUP)
+                for g in range(EARLY):
+                    load_positives(r, starts[g], WIDTHS[g])
             if r == 1:
                 nc.sync.dma_start(weights[:], w.rearrange("(r p) m -> p r m", p=P))
+        nc.gpsimd.memset(bias_rows[:], 0.0)
+        b_rows = b.rearrange("(m q i) one -> q m (i one)", q=P // BLOCK, i=BLOCK)
+        for q in range(P // BLOCK):
+            nc.sync.dma_start(bias_rows[q * BLOCK : q * BLOCK + MB, :], b_rows[q])
         for r in range(R):
-            load_positives(r, 2 * GROUP, N - 2 * GROUP)
+            load_positives(r, early_columns, N - early_columns)
 
         banks = {}
 
         def look_up(g, r):
-            cols = slice(g * GROUP, (g + 1) * GROUP)
-            diff = terms.tile([P, GROUP], F32)
+            width = WIDTHS[g]
+            cols = slice(starts[g], starts[g] + width)
+            diff = terms.tile([P, width], F32)
             nc.vector.tensor_tensor(
                 diff[:],
-                tables[r][:].indirect(offsets[:, g * GROUP // 16 : (g + 1) * GROUP // 16]),
+                tables[r][:].indirect(offsets[:, starts[g] // 16 : (starts[g] + width) // 16]),
                 positives[r][:, cols],
                 subtract,
             )
-            x = terms.tile([P, GROUP], BF16, bufs=16)
+            x = terms.tile([P, width], BF16, bufs=16)
             nc.scalar.activation(x[:], diff[:], Relu, bias=margin[:])
             for m in range(MB):
                 if r == 0:
-                    banks[g, m] = psum.tile([P, GROUP], F32, name=f"bank{g}_{m}", tag="bank")
+                    banks[g, m] = psum.tile([P, width], F32, name=f"bank{g}_{m}", tag="bank")
                 nc.tensor.matmul(
                     banks[g, m][:], weights[:, r, m * P : (m + 1) * P], x[:], start=r == 0, stop=r == R - 1
                 )
 
         def finish(g, m):
-            result = results.tile([P, GROUP], F32)
+            result = results.tile([P, WIDTHS[g]], F32)
             if m == MB - 1 or (g == G - 1 and m == 1):
                 nc.vector.tensor_scalar(result[:], banks[g, m][:], bias[:, m : m + 1], 0.0, add, maximum)
             else:
                 nc.scalar.activation(result[:], banks[g, m][:], Relu, bias=bias[:, m : m + 1])
-            nc.sync.dma_start(out[m * P : (m + 1) * P, g * GROUP : (g + 1) * GROUP], result[:])
+            nc.sync.dma_start(out[m * P : (m + 1) * P, starts[g] : starts[g] + WIDTHS[g]], result[:])
 
-        order = [(g, r) for r in range(R) for g in (0, 1)] + [(g, r) for g in range(2, G) for r in range(R)]
-        waiting = []
-        for i, (g, r) in enumerate(order):
-            for tile in waiting[:2]:
-                finish(*tile)
-            waiting = waiting[2:]
-            look_up(g, r)
-            if i > 0 and order[i - 1][1] == R - 1:
-                waiting += [(order[i - 1][0], m) for m in range(MB)]
+        for r in range(R):
+            for g in range(EARLY):
+                look_up(g, r)
+        nc.vector.transpose(bias[:], bias_rows[:])
+
+        waiting = [(g, m) for g in range(EARLY - 1) for m in range(MB)]
+        for g in range(EARLY, G):
+            for r in range(R):
+                for tile in waiting[:2]:
+                    finish(*tile)
+                waiting = waiting[2:]
+                look_up(g, r)
+                if r == LAG - 1:
+                    waiting += [(g - 1, m) for m in range(MB)]
         waiting += [(G - 1, m) for m in range(MB)]
         for tile in waiting:
             finish(*tile)

@@ -8,7 +8,6 @@ P = 128
 BANK = 512
 WIDTHS = (BANK, BANK, BANK, BANK // 2, BANK // 2)
 EARLY = 2
-BLOCK = 32
 LAG = 2
 MARGIN = 0.5
 FLOPS = 2 * 512 * 512 * 2048
@@ -26,13 +25,13 @@ def tile_lookup_hinge_sub_relu_kernel(tc, tab, pos, w, b, offs, out):
         tc.tile_pool(name="terms", bufs=4) as terms,
         tc.tile_pool(name="results", bufs=8) as results,
         tc.psum_pool(name="psum", bufs=8) as psum,
+        nc.allow_non_contiguous_dma(reason="the bias is loaded one value to a partition"),
     ):
         offsets = held.tile([P, N // 16], U16, name="offsets")
         tables = [held.tile([P, S], F32, name=f"table{r}") for r in range(R)]
         positives = [held.tile([P, N], F32, name=f"positives{r}") for r in range(R)]
         weights = held.tile([P, R, M], BF16, name="weights")
-        bias_rows = held.tile([P, BLOCK], F32, name="bias_rows", align_bytes=64)
-        bias = held.tile([P, BLOCK], F32, name="bias", align_bytes=64)
+        bias = held.tile([P, MB], F32, name="bias")
         margin = held.tile([P, 1], F32, name="margin")
         nc.gpsimd.memset(margin[:], MARGIN)
 
@@ -50,12 +49,10 @@ def tile_lookup_hinge_sub_relu_kernel(tc, tab, pos, w, b, offs, out):
                     load_positives(r, starts[g], WIDTHS[g])
             if r == 1:
                 nc.sync.dma_start(weights[:], w.rearrange("(r p) m -> p r m", p=P))
-        nc.gpsimd.memset(bias_rows[:], 0.0)
-        b_rows = b.rearrange("(m q i) one -> q m (i one)", q=P // BLOCK, i=BLOCK)
-        for q in range(P // BLOCK):
-            nc.sync.dma_start(bias_rows[q * BLOCK : q * BLOCK + MB, :], b_rows[q])
         for r in range(R):
             load_positives(r, early_columns, N - early_columns)
+            if r == 0:
+                nc.sync.dma_start(bias[:], b.rearrange("(m p) one -> p (m one)", p=P))
 
         banks = {}
 
@@ -89,7 +86,6 @@ def tile_lookup_hinge_sub_relu_kernel(tc, tab, pos, w, b, offs, out):
         for r in range(R):
             for g in range(EARLY):
                 look_up(g, r)
-        nc.vector.transpose(bias[:], bias_rows[:])
 
         waiting = [(g, m) for g in range(EARLY - 1) for m in range(MB)]
         for g in range(EARLY, G):

import concourse.mybir as mybir

F32, BF16, U16 = mybir.dt.float32, mybir.dt.bfloat16, mybir.dt.uint16
subtract, add, maximum = mybir.AluOpType.subtract, mybir.AluOpType.add, mybir.AluOpType.max
Relu = mybir.ActivationFunctionType.Relu

P = 128
BANK = 512
WIDTHS = (BANK, BANK, BANK, BANK // 2, BANK // 2)
EARLY = 2
LAG = 2
MARGIN = 0.5
FLOPS = 2 * 512 * 512 * 2048


def tile_lookup_hinge_sub_relu_kernel(tc, tab, pos, w, b, offs, out):
    nc = tc.nc
    K, S = tab.shape
    M, N = out.shape
    R, MB, G = K // P, M // P, len(WIDTHS)
    starts = [sum(WIDTHS[:g]) for g in range(G)]
    early_columns = starts[EARLY]
    with (
        tc.tile_pool(name="held", bufs=1) as held,
        tc.tile_pool(name="terms", bufs=4) as terms,
        tc.tile_pool(name="results", bufs=8) as results,
        tc.psum_pool(name="psum", bufs=8) as psum,
        nc.allow_non_contiguous_dma(reason="the bias is loaded one value to a partition"),
    ):
        offsets = held.tile([P, N // 16], U16, name="offsets")
        tables = [held.tile([P, S], F32, name=f"table{r}") for r in range(R)]
        positives = [held.tile([P, N], F32, name=f"positives{r}") for r in range(R)]
        weights = held.tile([P, R, M], BF16, name="weights")
        bias = held.tile([P, MB], F32, name="bias")
        margin = held.tile([P, 1], F32, name="margin")
        nc.gpsimd.memset(margin[:], MARGIN)

        def load_positives(r, start, width):
            cols = slice(start, start + width)
            nc.sync.dma_start(positives[r][:, cols], pos[r * P : (r + 1) * P, cols])

        nc.sync.dma_start(offsets[:], offs)
        for r in range(R):
            nc.sync.dma_start(tables[r][:], tab[r * P : (r + 1) * P, :])
            if r < R - 1:
                load_positives(r, 0, early_columns)
            else:
                for g in range(EARLY):
                    load_positives(r, starts[g], WIDTHS[g])
            if r == 1:
                nc.sync.dma_start(weights[:], w.rearrange("(r p) m -> p r m", p=P))
        for r in range(R):
            load_positives(r, early_columns, N - early_columns)
            if r == 0:
                nc.sync.dma_start(bias[:], b.rearrange("(m p) one -> p (m one)", p=P))

        banks = {}

        def look_up(g, r):
            width = WIDTHS[g]
            cols = slice(starts[g], starts[g] + width)
            diff = terms.tile([P, width], F32)
            nc.vector.tensor_tensor(
                diff[:],
                tables[r][:].indirect(offsets[:, starts[g] // 16 : (starts[g] + width) // 16]),
                positives[r][:, cols],
                subtract,
            )
            x = terms.tile([P, width], BF16, bufs=16)
            nc.scalar.activation(x[:], diff[:], Relu, bias=margin[:])
            for m in range(MB):
                if r == 0:
                    banks[g, m] = psum.tile([P, width], F32, name=f"bank{g}_{m}", tag="bank")
                nc.tensor.matmul(
                    banks[g, m][:], weights[:, r, m * P : (m + 1) * P], x[:], start=r == 0, stop=r == R - 1
                )

        def finish(g, m):
            result = results.tile([P, WIDTHS[g]], F32)
            if m == MB - 1 or (g == G - 1 and m == 1):
                nc.vector.tensor_scalar(result[:], banks[g, m][:], bias[:, m : m + 1], 0.0, add, maximum)
            else:
                nc.scalar.activation(result[:], banks[g, m][:], Relu, bias=bias[:, m : m + 1])
            nc.sync.dma_start(out[m * P : (m + 1) * P, starts[g] : starts[g] + WIDTHS[g]], result[:])

        for r in range(R):
            for g in range(EARLY):
                look_up(g, r)

        waiting = [(g, m) for g in range(EARLY - 1) for m in range(MB)]
        for g in range(EARLY, G):
            for r in range(R):
                for tile in waiting[:2]:
                    finish(*tile)
                waiting = waiting[2:]
                look_up(g, r)
                if r == LAG - 1:
                    waiting += [(g - 1, m) for m in range(MB)]
        waiting += [(G - 1, m) for m in range(MB)]
        for tile in waiting:
            finish(*tile)
